import numpy as np
import ml_dtypes


def mxq(x, axis, fmt="e4m3"):
    dtype, down = {"e4m3": (ml_dtypes.float8_e4m3fn, 7), "e5m2": (ml_dtypes.float8_e5m2, 14)}[fmt]
    v = np.moveaxis(np.asarray(x, np.float32).astype(ml_dtypes.bfloat16).astype(np.float64), axis, -1)
    blocks = v.reshape(v.shape[:-1] + (-1, 32))
    amax = np.abs(blocks).max(-1, keepdims=True)
    byte = np.maximum(np.where(amax > 0, np.frexp(amax)[1] - 1 + 127, 0) - down, 1)
    scale = np.exp2(byte - 127.0)
    codes = (blocks / scale).astype(np.float32).astype(dtype).astype(np.float64)
    return np.moveaxis((codes * scale).reshape(v.shape), -1, axis)


WIDE = False


def mx_kscale(k):
    if not WIDE:
        return np.ones(k)
    levels = np.array([10, -10, 5, -5, 0])
    if k % 512:
        return np.exp2(np.random.permutation(np.resize(levels, k // 32))).repeat(32)
    a = np.empty((k // 512, 16))
    for p in range(k // 512):
        a[p, :8] = np.random.permutation(np.resize(levels, 8))
        for g in range(8):
            far = levels[np.abs(levels - a[p, g]) >= 10]
            a[p, g + 8] = far[np.random.randint(len(far))]
    return np.exp2(a.ravel()).repeat(32)


BF16 = ml_dtypes.bfloat16


def bf(x):
    return np.asarray(x, np.float32).astype(BF16)


def f64(x):
    return np.asarray(x).astype(np.float64)


E2M1 = np.array([0.0, 0.5, 1.0, 1.5, 2.0, 3.0, 4.0, 6.0, -0.0, -0.5, -1.0, -1.5, -2.0, -3.0, -4.0, -6.0])


def pack_weight(w, fmt):
    k, n = w.shape
    w = f64(bf(w)).reshape(k // 32, 32, n)
    amax = np.abs(w).max(1)
    if fmt == "e4m3":
        byte = np.frexp(amax)[1] - 1 + 127 - 7
    else:
        mant, ex = np.frexp(amax / 6.0)
        byte = np.where(mant > 0.5, ex, ex - 1) + 127
    byte = np.clip(np.where(amax > 0, byte, 1), 1, 254)
    scaled = (w * np.exp2(127.0 - byte)[:, None, :]).reshape(k, n).astype(np.float32)
    by_word = np.ascontiguousarray(scaled.reshape(k // 512, 128, 4, n).transpose(0, 1, 3, 2))
    if fmt == "e4m3":
        words = by_word.astype(ml_dtypes.float8_e4m3fn).view(np.uint8)
    else:
        c = by_word.astype(ml_dtypes.float4_e2m1fn).view(np.uint8) & 0xF
        words = c[..., 0::2] | (c[..., 1::2] << 4)
    return np.ascontiguousarray(words), np.ascontiguousarray(byte.astype(np.uint8).reshape(k // 512, 16, n))


def unpack_weight(words, scales, fmt):
    g, p, n, _ = words.shape
    if fmt == "e4m3":
        vals = np.ascontiguousarray(words).view(ml_dtypes.float8_e4m3fn).astype(np.float64)
    else:
        nib = np.empty((g, p, n, 4), np.uint8)
        nib[..., 0::2] = words & 0xF
        nib[..., 1::2] = words >> 4
        vals = E2M1[nib]
    vals = vals * np.repeat(np.exp2(scales.astype(np.float64) - 127.0), 8, axis=1)[..., None]
    return vals.transpose(0, 1, 3, 2).reshape(g * 512, n)
def pack4(w):
    words, scales = pack_weight(w, "e2m1")
    return words.reshape(words.shape[0], 128, -1), scales


def unpack4(words, scales):
    return unpack_weight(words.reshape(words.shape[0], 128, -1, 2), scales, "e2m1")


M, D, G, F, C = 2048, 1024, 2, 512, 512
TAU = 0.1


def draw0():
    s = mx_kscale(D)
    t = np.stack([mx_kscale(F) for _ in range(G)])
    x = np.random.standard_normal((M, D)) * s
    proj = np.random.standard_normal((D, G * F)) / np.sqrt(D) / s[:, None]
    b = 0.3 * np.random.standard_normal((G, F))
    gain = 1 + 0.1 * np.random.standard_normal((G, F))
    codes = np.random.standard_normal((G, F, C)) / np.sqrt(F) * np.exp(0.2 * np.random.standard_normal((G, 1, C)))
    rlen = 1 / np.sqrt(np.sum((gain[:, :, None] * codes) ** 2, axis=1))
    prior = 0.2 * np.random.standard_normal((G, C))
    proj_words, proj_scales = pack4(proj)
    code_words, code_scales = pack_weight((codes / t[:, :, None]).transpose(1, 0, 2).reshape(F, G * C), "e4m3")
    return {"x": bf(x),
            "proj_words": proj_words, "proj_scales": proj_scales,
            "b": bf(b),
            "gain": bf(gain * t),
            "code_words": code_words, "code_scales": code_scales,
            "rlen": bf(rlen),
            "prior": bf(prior)}


def core(x, proj_words, proj_scales, b, gain, code_words, code_scales, rlen, prior):
    h = mxq(f64(x), 1, "e4m3") @ unpack4(proj_words, proj_scales)
    h = h.reshape(M, G, F) + f64(b)
    u = h / np.sqrt(np.mean(h * h, axis=2, keepdims=True)) * f64(gain)
    e = unpack_weight(code_words, code_scales, "e4m3")
    dots = np.stack([(mxq(u[:, i], 1, "e4m3") @ e[:, i * C:(i + 1) * C]) for i in range(G)])
    return dots * f64(rlen)[:, None, :] / (TAU * np.sqrt(F)) + f64(prior)[:, None, :]


def e4m3fn_bytes(y):
    return np.clip(np.asarray(y, np.float64), -448.0, 448.0).astype(np.float32).astype(ml_dtypes.float8_e4m3fn).view(np.uint8)


def e4m3fn_values(b):
    return np.asarray(b, np.uint8).view(ml_dtypes.float8_e4m3fn).astype(np.float64)


def setup_inputs():
    d = draw0()
    x0 = np.asarray(d['x']).astype(np.float64)
    s = (np.max(np.abs(x0), axis=(0,), keepdims=True) / 448.0).astype(np.float32)
    out = {}
    for k, v in d.items():
        if k == 'x':
            out['x_bytes'] = e4m3fn_bytes(x0 / s.astype(np.float64))
            out['x_scale'] = s
        else:
            out[k] = v
    return out


def reference(x_bytes, x_scale, proj_words, proj_scales, b, gain, code_words, code_scales, rlen, prior):
    return core(e4m3fn_values(x_bytes) * x_scale.astype(np.float64), proj_words, proj_scales, b, gain, code_words, code_scales, rlen, prior)

@@ -1,0 +1,322 @@
+import math
+from contextlib import ExitStack
+
+import concourse.mybir as mybir
+from concourse.masks import make_identity
+
+M, D, G, F, C = 2048, 1024, 2, 512, 512
+TAU = 0.1
+P = 128
+FLOPS = 2 * M * D * G * F + 2 * M * F * C * G
+
+F32 = mybir.dt.float32
+BF16 = mybir.dt.bfloat16
+U32 = mybir.dt.uint32
+I32 = mybir.dt.int32
+U8 = mybir.dt.uint8
+FP8 = mybir.dt.float8_e4m3fn
+FP8X4 = mybir.dt.float8_e4m3fn_x4
+FP4X4 = mybir.dt.float4_e2m1fn_x4
+ACT = mybir.ActivationFunctionType
+ALU = mybir.AluOpType
+ENG = mybir.EngineType
+
+N_TILES = M // P
+LOADS = (1, 1, 2, 4, 4, 4)
+TABLE = [("S3a", 5), ("M1a", -1), ("SQa", 0), ("T3a", 6), ("X1", -2), ("prod", -3), ("X3b", 6), ("T2", 3), ("M2b", 4), ("V3b", 2), ("V2a", -1), ("Q1", -2), ("X3a", 6), ("M1b", -1), ("X2", 3), ("M2a", 4), ("V3a", 2), ("SQb", 0), ("S3b", 4), ("V2b", -1), ("Q2", 3), ("T3b", 5), ("T1", -3), ("RS", 0)]
+ON_VECTOR = {"X3a": (13, 1), "X3b": (0, 3), "X1": (10, 4), "X2": (8, 1), "S3a": (14, 3), "S3b": (0, 0)}
+
+
+def on_vector(stage, n):
+    first, every = ON_VECTOR[stage]
+    return every > 0 and n >= first and n % every == every - 1
+
+
+def tile_hubert_codebook_logits_f7_kernel(
+    tc, x_bytes, x_scale, proj_words, proj_scales, b, gain, code_words, code_scales, rlen, prior, out
+):
+    nc = tc.nc
+    with ExitStack() as ctx:
+        keep = ctx.enter_context(tc.tile_pool(name="keep", bufs=1))
+        work = ctx.enter_context(tc.tile_pool(name="work", bufs=4))
+        vpool = ctx.enter_context(tc.tile_pool(name="vpool", bufs=14))
+        ps_x = ctx.enter_context(tc.psum_pool(name="ps_x", bufs=1))
+        ps_h = ctx.enter_context(tc.psum_pool(name="ps_h", bufs=2))
+        ps_u = ctx.enter_context(tc.psum_pool(name="ps_u", bufs=1))
+        ps_d = ctx.enter_context(tc.psum_pool(name="ps_d", bufs=2))
+        ps_o = ctx.enter_context(tc.psum_pool(name="ps_o", bufs=2))
+        ctx.enter_context(tc.manual_schedule(engines={ENG.PE, ENG.Activation, ENG.DVE}))
+
+        scale_bc = keep.tile([P, D], F32)
+        nc.scalar.dma_start(out=scale_bc[:], in_=x_scale.rearrange("o k -> (o k)").partition_broadcast(P))
+
+        warm = keep.tile([P, 1], F32)
+        warm_out = keep.tile([P, 1], F32)
+        nc.vector.memset(warm[:], 1.0)
+        nc.scalar.activation(out=warm_out[:], in_=warm[:], func=ACT.Abs_reciprocal_sqrt)
+
+        p_sc = keep.tile([P, 2, G * F], U8, align_bytes=64)
+        e_sc = keep.tile([P, G * C], U8, align_bytes=64)
+        nc.vector.memset(p_sc[:].rearrange("p g n -> p (g n)").bitcast(I32), 0)
+        nc.vector.memset(e_sc[:].bitcast(I32), 0)
+        ident = keep.tile([P, P], F32)
+        make_identity(nc, ident[:])
+
+        x_rows = x_bytes.rearrange("(p a) k -> p a k", a=N_TILES)
+        x_of_tile = []
+        first = 0
+        p_words = keep.tile([P, 2, 2 * G * F], U8, align_bytes=64)
+        e_words = keep.tile([P, 4 * G * C], U8, align_bytes=64)
+        for i, n in enumerate(LOADS):
+            codes_in = keep.tile([P, n, D], U8, name="x_in_%d" % i)
+            nc.sync.dma_start(out=codes_in[:], in_=x_rows[:, first : first + n, :])
+            for j in range(n):
+                x_of_tile.append((codes_in, j))
+            first += n
+            if i == 0:
+                for q in range(4):
+                    nc.sync.dma_start(
+                        out=p_sc[32 * q : 32 * q + 4, :, :].bitcast(I32),
+                        in_=proj_scales[:, 4 * q : 4 * q + 4, :].rearrange("g q n -> q g n").bitcast(I32),
+                    )
+                for g in range(2):
+                    nc.sync.dma_start(out=p_words[:, g, :].bitcast(I32), in_=proj_words[g].bitcast(I32))
+            if i == 2:
+                for q in range(4):
+                    nc.sync.dma_start(
+                        out=e_sc[32 * q : 32 * q + 4, :].bitcast(I32),
+                        in_=code_scales[0, 4 * q : 4 * q + 4, :].bitcast(I32),
+                    )
+                nc.sync.dma_start(
+                    out=e_words[:].bitcast(I32),
+                    in_=code_words[0].rearrange("p n t -> p (n t)").bitcast(I32),
+                )
+
+        b_bc = keep.tile([P, G, F], BF16)
+        nc.scalar.dma_start(out=b_bc[:], in_=b.rearrange("h f -> (h f)").partition_broadcast(P))
+        gain_in = keep.tile([P, G, F], BF16)
+        nc.scalar.dma_start(out=gain_in[:], in_=gain.rearrange("h f -> (h f)").partition_broadcast(P))
+        tail_in = keep.tile([P, P], BF16)
+        nc.gpsimd.memset(tail_in[:], 0.0)
+        nc.scalar.dma_start(out=tail_in[0:8, :], in_=rlen.rearrange("h (c j) -> (h c) j", j=P))
+        nc.scalar.dma_start(out=tail_in[8:16, :], in_=prior.rearrange("h (c j) -> (h c) j", j=P))
+
+        gain_bc = keep.tile([P, G, 2, P, 2], BF16)
+        rl = keep.tile([P, 8], F32)
+        pr = keep.tile([P, 8], F32)
+
+        def constants():
+            for h in range(G):
+                nc.vector.tensor_copy(
+                    out=gain_bc[:, h], in_=gain_in[:, h, :].rearrange("p (q u e) -> p u q e", u=2, e=2)
+                )
+            tail_f = keep.tile([P, P], F32)
+            nc.vector.tensor_copy(out=tail_f[:], in_=tail_in[:])
+            tail_t = ps_o.tile([P, 4, P], F32, name="oT")
+            nc.tensor.transpose(tail_t[:, 0, :], tail_f[:], ident[:])
+            nc.vector.tensor_scalar(
+                out=rl[:], in0=tail_t[:, 0, 0:8], scalar1=1.0 / (TAU * math.sqrt(F)), scalar2=None, op0=ALU.mult
+            )
+            nc.vector.tensor_copy(out=pr[:], in_=tail_t[:, 0, 8:16])
+
+        st = {}
+
+        def copy_out(stage, n, dst, src):
+            if on_vector(stage, n):
+                nc.vector.tensor_copy(out=dst, in_=src)
+            else:
+                nc.scalar.copy(out=dst, in_=src)
+
+        def prod(n):
+            codes_in, row = x_of_tile[n]
+            xs = work.tile([P, D], BF16, align_bytes=64)
+            nc.vector.tensor_tensor(out=xs[:], in0=codes_in[:, row, :].bitcast(FP8), in1=scale_bc[:], op=ALU.mult)
+            st["xs", n] = xs
+
+        def turn_x(n):
+            words = st.pop(("xs", n))[:].bitcast(F32)
+            xT = ps_x.tile([P, 2, 2, P], F32)
+            for g in range(2):
+                for u in range(2):
+                    nc.tensor.transpose(xT[:, g, u, :], words[:, 256 * g + u : 256 * (g + 1) : 2], ident[:])
+            st["xT", n] = xT
+
+        def exit_x(n):
+            xg = work.tile([P, 2, P, 4], BF16, align_bytes=64)
+            copy_out("X1", n, xg[:].bitcast(F32), st.pop(("xT", n))[:].rearrange("p g u r -> p g r u"))
+            st["xg", n] = xg
+
+        def quant_x(n):
+            xc = work.tile([P, 2, P], U32, align_bytes=64)
+            xc_sc = work.tile([P, 2, P], U8, align_bytes=64)
+            nc.vector.quantize_mx(
+                out=xc[:].rearrange("p g r -> p (g r)").bitcast(FP8X4),
+                scales=xc_sc[:].rearrange("p g r -> p (g r)"),
+                in_=st.pop(("xg", n))[:].rearrange("p g r t -> p (g r t)"),
+            )
+            st["xc", n] = (xc, xc_sc)
+
+        def project(n, h):
+            xc, xc_sc = st["xc", n]
+            hp = ps_h.tile([P, F], F32)
+            for g in range(2):
+                nc.tensor.matmul_mx(
+                    out=hp[:],
+                    lhsT=xc[:, g, :].bitcast(FP8X4),
+                    lhsT_scale=xc_sc[:, g, :],
+                    rhs=p_words[:, g, 2 * F * h : 2 * F * (h + 1)].bitcast(FP4X4),
+                    rhs_scale=p_sc[:, g, F * h : F * (h + 1)],
+                    start=(g == 0),
+                    stop=(g == 1),
+                )
+            st["hp", n, h] = hp
+
+        def add_bias(n, h):
+            v = vpool.tile([P, 2, P, 2], F32)
+            nc.vector.tensor_tensor(
+                out=v[:],
+                in0=st.pop(("hp", n, h))[:].rearrange("p (q u e) -> p u q e", u=2, e=2),
+                in1=b_bc[:, h, :].rearrange("p (q u e) -> p u q e", u=2, e=2),
+                op=ALU.add,
+            )
+            st["v", n, h] = v
+
+        def square(n, h):
+            if ("sums", n // 2) not in st:
+                sums = work.tile([P, 4], F32)
+                st["sums", n // 2] = sums
+            sums = st["sums", n // 2]
+            col = 2 * (n % 2) + h
+            sq = work.tile([P, F], BF16)
+            nc.scalar.activation(
+                out=sq[:],
+                in_=st["v", n, h][:].rearrange("p u q e -> p (u q e)"),
+                func=ACT.Square,
+                accum_out=sums[:, col : col + 1],
+            )
+
+        def root(n):
+            if n % 2 == 1:
+                rinv = work.tile([P, 4], F32)
+                nc.scalar.activation(
+                    out=rinv[:], in_=st.pop(("sums", n // 2))[:], func=ACT.Abs_reciprocal_sqrt, scale=1.0 / F
+                )
+                st["rinv", n // 2] = rinv
+
+        def normalise(m, j):
+            s, h = m // 2, m % 2
+            un = work.tile([P, F], BF16, align_bytes=64, name="un%d" % j)
+            col = 2 * j + h
+            nc.vector.scalar_tensor_tensor(
+                out=un[:],
+                in0=st.pop(("v", 2 * s + j, h))[:].rearrange("p u q e -> p (u q e)"),
+                scalar=st["rinv", s][:, col : col + 1],
+                in1=gain_bc[:, h].rearrange("p u q e -> p (u q e)"),
+                op0=ALU.mult,
+                op1=ALU.mult,
+            )
+            st["un", m, j] = un
+
+        def turn_u(m):
+            uT = ps_u.tile([P, 2, 2, P], F32)
+            for j in range(2):
+                words = st.pop(("un", m, j))[:].bitcast(F32)
+                for u in range(2):
+                    nc.tensor.transpose(uT[:, j, u, :], words[:, P * u : P * (u + 1)], ident[:])
+            st["uT", m] = uT
+
+        def exit_u(m):
+            ug = work.tile([P, 2, P, 4], BF16, align_bytes=64)
+            copy_out("X2", m, ug[:].bitcast(F32), st.pop(("uT", m))[:].rearrange("p j u r -> p j r u"))
+            st["ug", m] = ug
+
+        def quant_u(m):
+            uc = work.tile([P, 2 * P], U32, align_bytes=64)
+            uc_sc = work.tile([P, 2 * P], U8, align_bytes=64)
+            nc.vector.quantize_mx(
+                out=uc[:].bitcast(FP8X4), scales=uc_sc[:], in_=st.pop(("ug", m))[:].rearrange("p j r t -> p (j r t)")
+            )
+            st["uc", m] = (uc, uc_sc)
+
+        def compare(m, half):
+            uc, uc_sc = st["uc", m]
+            dp = ps_d.tile([P, 2, 2 * P], F32)
+            for i in range(2):
+                n0 = C * (m % 2) + P * (2 * half + i)
+                nc.tensor.matmul_mx(
+                    out=dp[:, i, :],
+                    lhsT=e_words[:, 4 * n0 : 4 * (n0 + P)].bitcast(FP8X4),
+                    lhsT_scale=e_sc[:, n0 : n0 + P],
+                    rhs=uc[:].bitcast(FP8X4),
+                    rhs_scale=uc_sc[:],
+                    start=True,
+                    stop=True,
+                )
+            st["dp", m, half] = dp
+
+        def scale_out(m, half):
+            if ("dots", m) not in st:
+                dots = work.tile([P, 4, 2 * P], F32)
+                st["dots", m] = dots
+            dots = st["dots", m]
+            dp = st.pop(("dp", m, half))
+            for i in range(2):
+                c = 2 * half + i
+                k = 4 * (m % 2) + c
+                if on_vector("S3" + "ab"[half], m):
+                    nc.vector.tensor_scalar(
+                        out=dots[:, c, :],
+                        in0=dp[:, i, :],
+                        scalar1=rl[:, k : k + 1],
+                        scalar2=pr[:, k : k + 1],
+                        op0=ALU.mult,
+                        op1=ALU.add,
+                    )
+                else:
+                    nc.scalar.activation(
+                        out=dots[:, c, :],
+                        in_=dp[:, i, :],
+                        func=ACT.Identity,
+                        scale=rl[:, k : k + 1],
+                        bias=pr[:, k : k + 1],
+                    )
+
+        def turn_out(m, j):
+            oT = ps_o.tile([P, 4, P], F32)
+            for c in range(4):
+                nc.tensor.transpose(oT[:, c, :], st["dots", m][:, c, P * j : P * (j + 1)], ident[:])
+            st["oT", m, j] = oT
+
+        def exit_out(m, j):
+            if ("o", m) not in st:
+                o_sb = work.tile([P, 2, C], F32)
+                st["o", m] = [o_sb, 0]
+            o_sb = st["o", m][0]
+            copy_out("X3" + "ab"[j], m, o_sb[:, j, :], st.pop(("oT", m, j))[:].rearrange("p c j -> p (c j)"))
+            st["o", m][1] += 1
+            if st["o", m][1] == 2:
+                s, h = m // 2, m % 2
+                nc.sync.dma_start(
+                    out=out[h].rearrange("(p a) c -> p a c", a=N_TILES)[:, 2 * s : 2 * s + 2, :], in_=o_sb[:]
+                )
+
+        run = {
+            "prod": prod, "T1": turn_x, "X1": exit_x, "Q1": quant_x,
+            "M1a": lambda n: project(n, 0), "M1b": lambda n: project(n, 1),
+            "V2a": lambda n: add_bias(n, 0), "V2b": lambda n: add_bias(n, 1),
+            "SQa": lambda n: square(n, 0), "SQb": lambda n: square(n, 1),
+            "RS": root,
+            "V3a": lambda m: normalise(m, 0), "V3b": lambda m: normalise(m, 1),
+            "T2": turn_u, "X2": exit_u, "Q2": quant_u,
+            "M2a": lambda m: compare(m, 0), "M2b": lambda m: compare(m, 1),
+            "S3a": lambda m: scale_out(m, 0), "S3b": lambda m: scale_out(m, 1),
+            "T3a": lambda m: turn_out(m, 0), "T3b": lambda m: turn_out(m, 1),
+            "X3a": lambda m: exit_out(m, 0), "X3b": lambda m: exit_out(m, 1),
+        }
+        lags = [lag for name, lag in TABLE]
+        for it in range(min(lags), N_TILES + max(lags)):
+            if it == 1:
+                constants()
+            for name, lag in TABLE:
+                if 0 <= it - lag < N_TILES:
+                    run[name](it - lag)

@@ -23,8 +23,9 @@ ENG = mybir.EngineType
 
 N_TILES = M // P
 LOADS = (1, 1, 2, 4, 4, 4)
-TABLE = [("S3a", 5), ("M1a", -1), ("SQa", 0), ("T3a", 6), ("X1", -2), ("prod", -3), ("X3b", 6), ("T2", 3), ("M2b", 4), ("V3b", 2), ("V2a", -1), ("Q1", -2), ("X3a", 6), ("M1b", -1), ("X2", 3), ("M2a", 4), ("V3a", 2), ("SQb", 0), ("S3b", 4), ("V2b", -1), ("Q2", 3), ("T3b", 5), ("T1", -3), ("RS", 0)]
-ON_VECTOR = {"X3a": (13, 1), "X3b": (0, 3), "X1": (10, 4), "X2": (8, 1), "S3a": (14, 3), "S3b": (0, 0)}
+LATE_SCALE = 2
+TABLE = [("SQa", 1), ("T3a", 7), ("RS", 2), ("T1", -1), ("T2", 4), ("S3a", 6), ("V2b", 1), ("X1", -1), ("X3b", 7), ("M2b", 5), ("M1a", 0), ("V2a", 0), ("V3a", 3), ("V3b", 3), ("X3a", 7), ("M2a", 5), ("T3b", 6), ("M1b", 0), ("X2", 4), ("S3b", 5), ("SQb", 1), ("Q2", 4), ("Q1", -1), ("prod", -3)]
+ON_VECTOR = {"X3a": (12, 2), "X3b": (14, 3), "X1": (15, 1), "X2": (2, 2), "S3a": (4, 0), "S3b": (10, 1)}
 
 
 def on_vector(stage, n):
@@ -47,8 +48,13 @@ def tile_hubert_codebook_logits_f7_kernel(
         ps_o = ctx.enter_context(tc.psum_pool(name="ps_o", bufs=2))
         ctx.enter_context(tc.manual_schedule(engines={ENG.PE, ENG.Activation, ENG.DVE}))
 
-        scale_bc = keep.tile([P, D], F32)
-        nc.scalar.dma_start(out=scale_bc[:], in_=x_scale.rearrange("o k -> (o k)").partition_broadcast(P))
+        scale_kp = keep.tile([P, 2, 4], F32)
+        nc.scalar.dma_start(out=scale_kp[:], in_=x_scale.rearrange("o (g p t) -> p (o g) t", p=P, t=4))
+
+        rows_in = keep.tile([P, G * F], BF16)
+        nc.vector.memset(rows_in[:], 0.0)
+        nc.scalar.dma_start(out=rows_in[0:1, :], in_=b.rearrange("(o h) f -> o (h f)", o=1))
+        nc.scalar.dma_start(out=rows_in[1:2, :], in_=gain.rearrange("(o h) f -> o (h f)", o=1))
 
         warm = keep.tile([P, 1], F32)
         warm_out = keep.tile([P, 1], F32)
@@ -61,6 +67,8 @@ def tile_hubert_codebook_logits_f7_kernel(
         nc.vector.memset(e_sc[:].bitcast(I32), 0)
         ident = keep.tile([P, P], F32)
         make_identity(nc, ident[:])
+        ident_b = keep.tile([P, P], BF16)
+        nc.vector.tensor_copy(out=ident_b[:], in_=ident[:])
 
         x_rows = x_bytes.rearrange("(p a) k -> p a k", a=N_TILES)
         x_of_tile = []
@@ -92,24 +100,45 @@ def tile_hubert_codebook_logits_f7_kernel(
                     in_=code_words[0].rearrange("p n t -> p (n t)").bitcast(I32),
                 )
 
-        b_bc = keep.tile([P, G, F], BF16)
-        nc.scalar.dma_start(out=b_bc[:], in_=b.rearrange("h f -> (h f)").partition_broadcast(P))
-        gain_in = keep.tile([P, G, F], BF16)
-        nc.scalar.dma_start(out=gain_in[:], in_=gain.rearrange("h f -> (h f)").partition_broadcast(P))
         tail_in = keep.tile([P, P], BF16)
         nc.gpsimd.memset(tail_in[:], 0.0)
         nc.scalar.dma_start(out=tail_in[0:8, :], in_=rlen.rearrange("h (c j) -> (h c) j", j=P))
         nc.scalar.dma_start(out=tail_in[8:16, :], in_=prior.rearrange("h (c j) -> (h c) j", j=P))
 
+        b_bc = keep.tile([P, G, 2, P, 2], BF16)
         gain_bc = keep.tile([P, G, 2, P, 2], BF16)
+        scale_bc = keep.tile([P, D], F32)
+
+        def spread_row(row, h, pool, name):
+            bank = pool.tile([P, F], F32, name=name)
+            nc.tensor.matmul(
+                bank[:],
+                lhsT=ident_b[:, row : row + 1].to_broadcast([P, P]),
+                rhs=rows_in[:, F * h : F * (h + 1)],
+                start=True,
+                stop=True,
+            )
+            return bank[:].rearrange("p (q u e) -> p u q e", u=2, e=2)
+
+        for h in range(G):
+            nc.vector.tensor_copy(out=b_bc[:, h], in_=spread_row(0, h, ps_h, "hp"))
+
+        def spread_scale():
+            for g in range(2):
+                bank = ps_o.tile([P, 4, P], F32, name="oT")
+                for t in range(4):
+                    nc.tensor.transpose(bank[:, t, :], scale_kp[:, g, t : t + 1].to_broadcast([P, P]), ident[:])
+                nc.scalar.copy(
+                    out=scale_bc[:, F * g : F * (g + 1)].rearrange("p (q t) -> p q t", t=4),
+                    in_=bank[:].rearrange("p t q -> p q t"),
+                )
+
         rl = keep.tile([P, 8], F32)
         pr = keep.tile([P, 8], F32)
 
         def constants():
             for h in range(G):
-                nc.vector.tensor_copy(
-                    out=gain_bc[:, h], in_=gain_in[:, h, :].rearrange("p (q u e) -> p u q e", u=2, e=2)
-                )
+                nc.scalar.copy(out=gain_bc[:, h], in_=spread_row(1, h, ps_d, "dp"))
             tail_f = keep.tile([P, P], F32)
             nc.vector.tensor_copy(out=tail_f[:], in_=tail_in[:])
             tail_t = ps_o.tile([P, 4, P], F32, name="oT")
@@ -130,7 +159,11 @@ def tile_hubert_codebook_logits_f7_kernel(
         def prod(n):
             codes_in, row = x_of_tile[n]
             xs = work.tile([P, D], BF16, align_bytes=64)
-            nc.vector.tensor_tensor(out=xs[:], in0=codes_in[:, row, :].bitcast(FP8), in1=scale_bc[:], op=ALU.mult)
+            codes = codes_in[:, row, :].bitcast(FP8)
+            if n < LATE_SCALE:
+                nc.scalar.copy(out=xs[:], in_=codes)
+            else:
+                nc.vector.tensor_tensor(out=xs[:], in0=codes, in1=scale_bc[:], op=ALU.mult)
             st["xs", n] = xs
 
         def turn_x(n):
@@ -143,7 +176,17 @@ def tile_hubert_codebook_logits_f7_kernel(
 
         def exit_x(n):
             xg = work.tile([P, 2, P, 4], BF16, align_bytes=64)
-            copy_out("X1", n, xg[:].bitcast(F32), st.pop(("xT", n))[:].rearrange("p g u r -> p g r u"))
+            xT = st.pop(("xT", n))
+            if n < LATE_SCALE:
+                for g in range(2):
+                    nc.vector.tensor_tensor(
+                        out=xg[:, g].rearrange("p r (u e) -> p r u e", e=2),
+                        in0=xT[:, g].bitcast(BF16).rearrange("p u (r e) -> p r u e", e=2),
+                        in1=scale_kp[:, g].rearrange("p (u e) -> p u e", e=2).unsqueeze(1).to_broadcast([P, P, 2, 2]),
+                        op=ALU.mult,
+                    )
+            else:
+                copy_out("X1", n, xg[:].bitcast(F32), xT[:].rearrange("p g u r -> p g r u"))
             st["xg", n] = xg
 
         def quant_x(n):
@@ -176,7 +219,7 @@ def tile_hubert_codebook_logits_f7_kernel(
             nc.vector.tensor_tensor(
                 out=v[:],
                 in0=st.pop(("hp", n, h))[:].rearrange("p (q u e) -> p u q e", u=2, e=2),
-                in1=b_bc[:, h, :].rearrange("p (q u e) -> p u q e", u=2, e=2),
+                in1=b_bc[:, h],
                 op=ALU.add,
             )
             st["v", n, h] = v
@@ -313,8 +356,11 @@ def tile_hubert_codebook_logits_f7_kernel(
             "T3a": lambda m: turn_out(m, 0), "T3b": lambda m: turn_out(m, 1),
             "X3a": lambda m: exit_out(m, 0), "X3b": lambda m: exit_out(m, 1),
         }
+        LAG = dict(TABLE)
         lags = [lag for name, lag in TABLE]
         for it in range(min(lags), N_TILES + max(lags)):
+            if it == LATE_SCALE + LAG["prod"]:
+                spread_scale()
             if it == 1:
                 constants()
             for name, lag in TABLE:

@@ -24,8 +24,8 @@ ENG = mybir.EngineType
 N_TILES = M // P
 LOADS = (1, 1, 2, 4, 4, 4)
 LATE_SCALE = 2
-TABLE = [("SQa", 1), ("T3a", 7), ("RS", 2), ("T1", -1), ("T2", 4), ("S3a", 6), ("V2b", 1), ("X1", -1), ("X3b", 7), ("M2b", 5), ("M1a", 0), ("V2a", 0), ("V3a", 3), ("V3b", 3), ("X3a", 7), ("M2a", 5), ("T3b", 6), ("M1b", 0), ("X2", 4), ("S3b", 5), ("SQb", 1), ("Q2", 4), ("Q1", -1), ("prod", -3)]
-ON_VECTOR = {"X3a": (12, 2), "X3b": (14, 3), "X1": (15, 1), "X2": (2, 2), "S3a": (4, 0), "S3b": (10, 1)}
+TABLE = [("SQa", 2), ("V3a", 4), ("V3b", 4), ("X1", 0), ("M2a", 6), ("T3a", 7), ("T3b", 7), ("SQb", 2), ("S3b", 6), ("M1b", 1), ("T2", 4), ("prod", -1), ("Q2", 5), ("X3a", 7), ("T1", -1), ("RS", 2), ("S3a", 6), ("X3b", 7), ("M2b", 5), ("V2a", 1), ("Q1", 0), ("X2", 4), ("M1a", 0), ("V2b", 1)]
+ON_VECTOR = {"X3a": (15, 0), "X3b": (13, 1), "X1": (12, 2), "X2": (13, 4), "S3a": (8, 1), "S3b": (2, 4)}
 
 
 def on_vector(stage, n):
@@ -120,8 +120,9 @@ def tile_hubert_codebook_logits_f7_kernel(
             )
             return bank[:].rearrange("p (q u e) -> p u q e", u=2, e=2)
 
-        for h in range(G):
-            nc.vector.tensor_copy(out=b_bc[:, h], in_=spread_row(0, h, ps_h, "hp"))
+        def spread_bias():
+            for h in range(G):
+                nc.scalar.copy(out=b_bc[:, h], in_=spread_row(0, h, ps_h, "hp"))
 
         def spread_scale():
             for g in range(2):
@@ -160,11 +161,16 @@ def tile_hubert_codebook_logits_f7_kernel(
             codes_in, row = x_of_tile[n]
             xs = work.tile([P, D], BF16, align_bytes=64)
             codes = codes_in[:, row, :].bitcast(FP8)
-            if n < LATE_SCALE:
+            if n == 0:
+                nc.vector.tensor_copy(out=xs[:], in_=codes)
+            elif n < LATE_SCALE:
                 nc.scalar.copy(out=xs[:], in_=codes)
             else:
                 nc.vector.tensor_tensor(out=xs[:], in0=codes, in1=scale_bc[:], op=ALU.mult)
             st["xs", n] = xs
+            if n == LATE_SCALE - 1:
+                spread_bias()
+                spread_scale()
 
         def turn_x(n):
             words = st.pop(("xs", n))[:].bitcast(F32)
@@ -202,15 +208,15 @@ def tile_hubert_codebook_logits_f7_kernel(
         def project(n, h):
             xc, xc_sc = st["xc", n]
             hp = ps_h.tile([P, F], F32)
-            for g in range(2):
+            for g, start, stop in ((0, True, True), (0, True, False), (1, False, True)):
                 nc.tensor.matmul_mx(
                     out=hp[:],
                     lhsT=xc[:, g, :].bitcast(FP8X4),
                     lhsT_scale=xc_sc[:, g, :],
                     rhs=p_words[:, g, 2 * F * h : 2 * F * (h + 1)].bitcast(FP4X4),
                     rhs_scale=p_sc[:, g, F * h : F * (h + 1)],
-                    start=(g == 0),
-                    stop=(g == 1),
+                    start=start,
+                    stop=stop,
                 )
             st["hp", n, h] = hp
 
@@ -337,11 +343,12 @@ def tile_hubert_codebook_logits_f7_kernel(
             o_sb = st["o", m][0]
             copy_out("X3" + "ab"[j], m, o_sb[:, j, :], st.pop(("oT", m, j))[:].rearrange("p c j -> p (c j)"))
             st["o", m][1] += 1
-            if st["o", m][1] == 2:
-                s, h = m // 2, m % 2
-                nc.sync.dma_start(
-                    out=out[h].rearrange("(p a) c -> p a c", a=N_TILES)[:, 2 * s : 2 * s + 2, :], in_=o_sb[:]
-                )
+            s, h = m // 2, m % 2
+            rows = out[h].rearrange("(p a) c -> p a c", a=N_TILES)
+            if m >= N_TILES - 2:
+                nc.sync.dma_start(out=rows[:, 2 * s + j, :], in_=o_sb[:, j, :])
+            elif st["o", m][1] == 2:
+                nc.sync.dma_start(out=rows[:, 2 * s : 2 * s + 2, :], in_=o_sb[:])
 
         run = {
             "prod": prod, "T1": turn_x, "X1": exit_x, "Q1": quant_x,
@@ -356,11 +363,8 @@ def tile_hubert_codebook_logits_f7_kernel(
             "T3a": lambda m: turn_out(m, 0), "T3b": lambda m: turn_out(m, 1),
             "X3a": lambda m: exit_out(m, 0), "X3b": lambda m: exit_out(m, 1),
         }
-        LAG = dict(TABLE)
         lags = [lag for name, lag in TABLE]
         for it in range(min(lags), N_TILES + max(lags)):
-            if it == LATE_SCALE + LAG["prod"]:
-                spread_scale()
             if it == 1:
                 constants()
             for name, lag in TABLE:

@@ -51,6 +51,8 @@ def tile_hubert_codebook_logits_f7_kernel(
         scale_kp = keep.tile([P, 2, 4], F32)
         nc.scalar.dma_start(out=scale_kp[:], in_=x_scale.rearrange("o (g p t) -> p (o g) t", p=P, t=4))
 
+        p_sc = keep.tile([P, 2, G * F], U8, align_bytes=64)
+        nc.vector.memset(p_sc[:].rearrange("p g n -> p (g n)").bitcast(I32), 0)
         rows_in = keep.tile([P, G * F], BF16)
         nc.vector.memset(rows_in[:], 0.0)
         nc.scalar.dma_start(out=rows_in[0:1, :], in_=b.rearrange("(o h) f -> o (h f)", o=1))
@@ -61,9 +63,7 @@ def tile_hubert_codebook_logits_f7_kernel(
         nc.vector.memset(warm[:], 1.0)
         nc.scalar.activation(out=warm_out[:], in_=warm[:], func=ACT.Abs_reciprocal_sqrt)
 
-        p_sc = keep.tile([P, 2, G * F], U8, align_bytes=64)
         e_sc = keep.tile([P, G * C], U8, align_bytes=64)
-        nc.vector.memset(p_sc[:].rearrange("p g n -> p (g n)").bitcast(I32), 0)
         nc.vector.memset(e_sc[:].bitcast(I32), 0)
         ident = keep.tile([P, P], F32)
         make_identity(nc, ident[:])
@@ -81,7 +81,7 @@ def tile_hubert_codebook_logits_f7_kernel(
             for j in range(n):
                 x_of_tile.append((codes_in, j))
             first += n
-            if i == 0:
+            if i == 1:
                 for q in range(4):
                     nc.sync.dma_start(
                         out=p_sc[32 * q : 32 * q + 4, :, :].bitcast(I32),
@@ -89,7 +89,7 @@ def tile_hubert_codebook_logits_f7_kernel(
                     )
                 for g in range(2):
                     nc.sync.dma_start(out=p_words[:, g, :].bitcast(I32), in_=proj_words[g].bitcast(I32))
-            if i == 2:
+            if i == 3:
                 for q in range(4):
                     nc.sync.dma_start(
                         out=e_sc[32 * q : 32 * q + 4, :].bitcast(I32),
@@ -137,17 +137,25 @@ def tile_hubert_codebook_logits_f7_kernel(
         rl = keep.tile([P, 8], F32)
         pr = keep.tile([P, 8], F32)
 
+        tail_f = keep.tile([P, P], F32)
+        early = {}
+
+        def spread_gain():
+            for h in range(G):
+                early["gain", h] = spread_row(1, h, ps_d, "dp")
+            nc.scalar.copy(out=tail_f[:], in_=tail_in[:])
+            tail_t = ps_u.tile([P, 2, 2, P], F32, name="uT")
+            nc.tensor.transpose(tail_t[:, 0, 0, :], tail_f[:], ident[:])
+            early["tail"] = tail_t
+
         def constants():
             for h in range(G):
-                nc.scalar.copy(out=gain_bc[:, h], in_=spread_row(1, h, ps_d, "dp"))
-            tail_f = keep.tile([P, P], F32)
-            nc.vector.tensor_copy(out=tail_f[:], in_=tail_in[:])
-            tail_t = ps_o.tile([P, 4, P], F32, name="oT")
-            nc.tensor.transpose(tail_t[:, 0, :], tail_f[:], ident[:])
-            nc.vector.tensor_scalar(
-                out=rl[:], in0=tail_t[:, 0, 0:8], scalar1=1.0 / (TAU * math.sqrt(F)), scalar2=None, op0=ALU.mult
+                nc.scalar.copy(out=gain_bc[:, h], in_=early["gain", h])
+            tail_t = early["tail"]
+            nc.scalar.activation(
+                out=rl[:], in_=tail_t[:, 0, 0, 0:8], func=ACT.Copy, scale=1.0 / (TAU * math.sqrt(F))
             )
-            nc.vector.tensor_copy(out=pr[:], in_=tail_t[:, 0, 8:16])
+            nc.scalar.copy(out=pr[:], in_=tail_t[:, 0, 0, 8:16])
 
         st = {}
 
@@ -171,6 +179,7 @@ def tile_hubert_codebook_logits_f7_kernel(
             if n == LATE_SCALE - 1:
                 spread_bias()
                 spread_scale()
+                spread_gain()
 
         def turn_x(n):
             words = st.pop(("xs", n))[:].bitcast(F32)
@@ -208,15 +217,15 @@ def tile_hubert_codebook_logits_f7_kernel(
         def project(n, h):
             xc, xc_sc = st["xc", n]
             hp = ps_h.tile([P, F], F32)
-            for g, start, stop in ((0, True, True), (0, True, False), (1, False, True)):
+            for g in range(2):
                 nc.tensor.matmul_mx(
                     out=hp[:],
                     lhsT=xc[:, g, :].bitcast(FP8X4),
                     lhsT_scale=xc_sc[:, g, :],
                     rhs=p_words[:, g, 2 * F * h : 2 * F * (h + 1)].bitcast(FP4X4),
                     rhs_scale=p_sc[:, g, F * h : F * (h + 1)],
-                    start=start,
-                    stop=stop,
+                    start=(g == 0),
+                    stop=(g == 1),
                 )
             st["hp", n, h] = hp
 

import math
from contextlib import ExitStack

import concourse.mybir as mybir
from concourse.masks import make_identity

M, D, G, F, C = 2048, 1024, 2, 512, 512
TAU = 0.1
P = 128
FLOPS = 2 * M * D * G * F + 2 * M * F * C * G

F32 = mybir.dt.float32
BF16 = mybir.dt.bfloat16
U32 = mybir.dt.uint32
I32 = mybir.dt.int32
U8 = mybir.dt.uint8
FP8 = mybir.dt.float8_e4m3fn
FP8X4 = mybir.dt.float8_e4m3fn_x4
FP4X4 = mybir.dt.float4_e2m1fn_x4
ACT = mybir.ActivationFunctionType
ALU = mybir.AluOpType
ENG = mybir.EngineType

N_TILES = M // P
LOADS = (1, 1, 2, 4, 4, 4)
LATE_SCALE = 2
TABLE = [("SQa", 2), ("V3a", 4), ("V3b", 4), ("X1", 0), ("M2a", 6), ("T3a", 7), ("T3b", 7), ("SQb", 2), ("S3b", 6), ("M1b", 1), ("T2", 4), ("prod", -1), ("Q2", 5), ("X3a", 7), ("T1", -1), ("RS", 2), ("S3a", 6), ("X3b", 7), ("M2b", 5), ("V2a", 1), ("Q1", 0), ("X2", 4), ("M1a", 0), ("V2b", 1)]
ON_VECTOR = {"X3a": (15, 0), "X3b": (13, 1), "X1": (12, 2), "X2": (13, 4), "S3a": (8, 1), "S3b": (2, 4)}


def on_vector(stage, n):
    first, every = ON_VECTOR[stage]
    return every > 0 and n >= first and n % every == every - 1


def tile_hubert_codebook_logits_f7_kernel(
    tc, x_bytes, x_scale, proj_words, proj_scales, b, gain, code_words, code_scales, rlen, prior, out
):
    nc = tc.nc
    with ExitStack() as ctx:
        keep = ctx.enter_context(tc.tile_pool(name="keep", bufs=1))
        work = ctx.enter_context(tc.tile_pool(name="work", bufs=4))
        vpool = ctx.enter_context(tc.tile_pool(name="vpool", bufs=14))
        ps_x = ctx.enter_context(tc.psum_pool(name="ps_x", bufs=1))
        ps_h = ctx.enter_context(tc.psum_pool(name="ps_h", bufs=2))
        ps_u = ctx.enter_context(tc.psum_pool(name="ps_u", bufs=1))
        ps_d = ctx.enter_context(tc.psum_pool(name="ps_d", bufs=2))
        ps_o = ctx.enter_context(tc.psum_pool(name="ps_o", bufs=2))
        ctx.enter_context(tc.manual_schedule(engines={ENG.PE, ENG.Activation, ENG.DVE}))

        scale_kp = keep.tile([P, 2, 4], F32)
        nc.scalar.dma_start(out=scale_kp[:], in_=x_scale.rearrange("o (g p t) -> p (o g) t", p=P, t=4))

        p_sc = keep.tile([P, 2, G * F], U8, align_bytes=64)
        nc.vector.memset(p_sc[:].rearrange("p g n -> p (g n)").bitcast(I32), 0)
        rows_in = keep.tile([P, G * F], BF16)
        nc.vector.memset(rows_in[:], 0.0)
        nc.scalar.dma_start(out=rows_in[0:1, :], in_=b.rearrange("(o h) f -> o (h f)", o=1))
        nc.scalar.dma_start(out=rows_in[1:2, :], in_=gain.rearrange("(o h) f -> o (h f)", o=1))

        warm = keep.tile([P, 1], F32)
        warm_out = keep.tile([P, 1], F32)
        nc.vector.memset(warm[:], 1.0)
        nc.scalar.activation(out=warm_out[:], in_=warm[:], func=ACT.Abs_reciprocal_sqrt)

        e_sc = keep.tile([P, G * C], U8, align_bytes=64)
        nc.vector.memset(e_sc[:].bitcast(I32), 0)
        ident = keep.tile([P, P], F32)
        make_identity(nc, ident[:])
        ident_b = keep.tile([P, P], BF16)
        nc.vector.tensor_copy(out=ident_b[:], in_=ident[:])

        x_rows = x_bytes.rearrange("(p a) k -> p a k", a=N_TILES)
        x_of_tile = []
        first = 0
        p_words = keep.tile([P, 2, 2 * G * F], U8, align_bytes=64)
        e_words = keep.tile([P, 4 * G * C], U8, align_bytes=64)
        for i, n in enumerate(LOADS):
            codes_in = keep.tile([P, n, D], U8, name="x_in_%d" % i)
            nc.sync.dma_start(out=codes_in[:], in_=x_rows[:, first : first + n, :])
            for j in range(n):
                x_of_tile.append((codes_in, j))
            first += n
            if i == 1:
                for q in range(4):
                    nc.sync.dma_start(
                        out=p_sc[32 * q : 32 * q + 4, :, :].bitcast(I32),
                        in_=proj_scales[:, 4 * q : 4 * q + 4, :].rearrange("g q n -> q g n").bitcast(I32),
                    )
                for g in range(2):
                    nc.sync.dma_start(out=p_words[:, g, :].bitcast(I32), in_=proj_words[g].bitcast(I32))
            if i == 3:
                for q in range(4):
                    nc.sync.dma_start(
                        out=e_sc[32 * q : 32 * q + 4, :].bitcast(I32),
                        in_=code_scales[0, 4 * q : 4 * q + 4, :].bitcast(I32),
                    )
                nc.sync.dma_start(
                    out=e_words[:].bitcast(I32),
                    in_=code_words[0].rearrange("p n t -> p (n t)").bitcast(I32),
                )

        tail_in = keep.tile([P, P], BF16)
        nc.gpsimd.memset(tail_in[:], 0.0)
        nc.scalar.dma_start(out=tail_in[0:8, :], in_=rlen.rearrange("h (c j) -> (h c) j", j=P))
        nc.scalar.dma_start(out=tail_in[8:16, :], in_=prior.rearrange("h (c j) -> (h c) j", j=P))

        b_bc = keep.tile([P, G, 2, P, 2], BF16)
        gain_bc = keep.tile([P, G, 2, P, 2], BF16)
        scale_bc = keep.tile([P, D], F32)

        def spread_row(row, h, pool, name):
            bank = pool.tile([P, F], F32, name=name)
            nc.tensor.matmul(
                bank[:],
                lhsT=ident_b[:, row : row + 1].to_broadcast([P, P]),
                rhs=rows_in[:, F * h : F * (h + 1)],
                start=True,
                stop=True,
            )
            return bank[:].rearrange("p (q u e) -> p u q e", u=2, e=2)

        def spread_bias():
            for h in range(G):
                nc.scalar.copy(out=b_bc[:, h], in_=spread_row(0, h, ps_h, "hp"))

        def spread_scale():
            for g in range(2):
                bank = ps_o.tile([P, 4, P], F32, name="oT")
                for t in range(4):
                    nc.tensor.transpose(bank[:, t, :], scale_kp[:, g, t : t + 1].to_broadcast([P, P]), ident[:])
                nc.scalar.copy(
                    out=scale_bc[:, F * g : F * (g + 1)].rearrange("p (q t) -> p q t", t=4),
                    in_=bank[:].rearrange("p t q -> p q t"),
                )

        rl = keep.tile([P, 8], F32)
        pr = keep.tile([P, 8], F32)

        tail_f = keep.tile([P, P], F32)
        early = {}

        def spread_gain():
            for h in range(G):
                early["gain", h] = spread_row(1, h, ps_d, "dp")
            nc.scalar.copy(out=tail_f[:], in_=tail_in[:])
            tail_t = ps_u.tile([P, 2, 2, P], F32, name="uT")
            nc.tensor.transpose(tail_t[:, 0, 0, :], tail_f[:], ident[:])
            early["tail"] = tail_t

        def constants():
            for h in range(G):
                nc.scalar.copy(out=gain_bc[:, h], in_=early["gain", h])
            tail_t = early["tail"]
            nc.scalar.activation(
                out=rl[:], in_=tail_t[:, 0, 0, 0:8], func=ACT.Copy, scale=1.0 / (TAU * math.sqrt(F))
            )
            nc.scalar.copy(out=pr[:], in_=tail_t[:, 0, 0, 8:16])

        st = {}

        def copy_out(stage, n, dst, src):
            if on_vector(stage, n):
                nc.vector.tensor_copy(out=dst, in_=src)
            else:
                nc.scalar.copy(out=dst, in_=src)

        def prod(n):
            codes_in, row = x_of_tile[n]
            xs = work.tile([P, D], BF16, align_bytes=64)
            codes = codes_in[:, row, :].bitcast(FP8)
            if n == 0:
                nc.vector.tensor_copy(out=xs[:], in_=codes)
            elif n < LATE_SCALE:
                nc.scalar.copy(out=xs[:], in_=codes)
            else:
                nc.vector.tensor_tensor(out=xs[:], in0=codes, in1=scale_bc[:], op=ALU.mult)
            st["xs", n] = xs
            if n == LATE_SCALE - 1:
                spread_bias()
                spread_scale()
                spread_gain()

        def turn_x(n):
            words = st.pop(("xs", n))[:].bitcast(F32)
            xT = ps_x.tile([P, 2, 2, P], F32)
            for g in range(2):
                for u in range(2):
                    nc.tensor.transpose(xT[:, g, u, :], words[:, 256 * g + u : 256 * (g + 1) : 2], ident[:])
            st["xT", n] = xT

        def exit_x(n):
            xg = work.tile([P, 2, P, 4], BF16, align_bytes=64)
            xT = st.pop(("xT", n))
            if n < LATE_SCALE:
                for g in range(2):
                    nc.vector.tensor_tensor(
                        out=xg[:, g].rearrange("p r (u e) -> p r u e", e=2),
                        in0=xT[:, g].bitcast(BF16).rearrange("p u (r e) -> p r u e", e=2),
                        in1=scale_kp[:, g].rearrange("p (u e) -> p u e", e=2).unsqueeze(1).to_broadcast([P, P, 2, 2]),
                        op=ALU.mult,
                    )
            else:
                copy_out("X1", n, xg[:].bitcast(F32), xT[:].rearrange("p g u r -> p g r u"))
            st["xg", n] = xg

        def quant_x(n):
            xc = work.tile([P, 2, P], U32, align_bytes=64)
            xc_sc = work.tile([P, 2, P], U8, align_bytes=64)
            nc.vector.quantize_mx(
                out=xc[:].rearrange("p g r -> p (g r)").bitcast(FP8X4),
                scales=xc_sc[:].rearrange("p g r -> p (g r)"),
                in_=st.pop(("xg", n))[:].rearrange("p g r t -> p (g r t)"),
            )
            st["xc", n] = (xc, xc_sc)

        def project(n, h):
            xc, xc_sc = st["xc", n]
            hp = ps_h.tile([P, F], F32)
            for g in range(2):
                nc.tensor.matmul_mx(
                    out=hp[:],
                    lhsT=xc[:, g, :].bitcast(FP8X4),
                    lhsT_scale=xc_sc[:, g, :],
                    rhs=p_words[:, g, 2 * F * h : 2 * F * (h + 1)].bitcast(FP4X4),
                    rhs_scale=p_sc[:, g, F * h : F * (h + 1)],
                    start=(g == 0),
                    stop=(g == 1),
                )
            st["hp", n, h] = hp

        def add_bias(n, h):
            v = vpool.tile([P, 2, P, 2], F32)
            nc.vector.tensor_tensor(
                out=v[:],
                in0=st.pop(("hp", n, h))[:].rearrange("p (q u e) -> p u q e", u=2, e=2),
                in1=b_bc[:, h],
                op=ALU.add,
            )
            st["v", n, h] = v

        def square(n, h):
            if ("sums", n // 2) not in st:
                sums = work.tile([P, 4], F32)
                st["sums", n // 2] = sums
            sums = st["sums", n // 2]
            col = 2 * (n % 2) + h
            sq = work.tile([P, F], BF16)
            nc.scalar.activation(
                out=sq[:],
                in_=st["v", n, h][:].rearrange("p u q e -> p (u q e)"),
                func=ACT.Square,
                accum_out=sums[:, col : col + 1],
            )

        def root(n):
            if n % 2 == 1:
                rinv = work.tile([P, 4], F32)
                nc.scalar.activation(
                    out=rinv[:], in_=st.pop(("sums", n // 2))[:], func=ACT.Abs_reciprocal_sqrt, scale=1.0 / F
                )
                st["rinv", n // 2] = rinv

        def normalise(m, j):
            s, h = m // 2, m % 2
            un = work.tile([P, F], BF16, align_bytes=64, name="un%d" % j)
            col = 2 * j + h
            nc.vector.scalar_tensor_tensor(
                out=un[:],
                in0=st.pop(("v", 2 * s + j, h))[:].rearrange("p u q e -> p (u q e)"),
                scalar=st["rinv", s][:, col : col + 1],
                in1=gain_bc[:, h].rearrange("p u q e -> p (u q e)"),
                op0=ALU.mult,
                op1=ALU.mult,
            )
            st["un", m, j] = un

        def turn_u(m):
            uT = ps_u.tile([P, 2, 2, P], F32)
            for j in range(2):
                words = st.pop(("un", m, j))[:].bitcast(F32)
                for u in range(2):
                    nc.tensor.transpose(uT[:, j, u, :], words[:, P * u : P * (u + 1)], ident[:])
            st["uT", m] = uT

        def exit_u(m):
            ug = work.tile([P, 2, P, 4], BF16, align_bytes=64)
            copy_out("X2", m, ug[:].bitcast(F32), st.pop(("uT", m))[:].rearrange("p j u r -> p j r u"))
            st["ug", m] = ug

        def quant_u(m):
            uc = work.tile([P, 2 * P], U32, align_bytes=64)
            uc_sc = work.tile([P, 2 * P], U8, align_bytes=64)
            nc.vector.quantize_mx(
                out=uc[:].bitcast(FP8X4), scales=uc_sc[:], in_=st.pop(("ug", m))[:].rearrange("p j r t -> p (j r t)")
            )
            st["uc", m] = (uc, uc_sc)

        def compare(m, half):
            uc, uc_sc = st["uc", m]
            dp = ps_d.tile([P, 2, 2 * P], F32)
            for i in range(2):
                n0 = C * (m % 2) + P * (2 * half + i)
                nc.tensor.matmul_mx(
                    out=dp[:, i, :],
                    lhsT=e_words[:, 4 * n0 : 4 * (n0 + P)].bitcast(FP8X4),
                    lhsT_scale=e_sc[:, n0 : n0 + P],
                    rhs=uc[:].bitcast(FP8X4),
                    rhs_scale=uc_sc[:],
                    start=True,
                    stop=True,
                )
            st["dp", m, half] = dp

        def scale_out(m, half):
            if ("dots", m) not in st:
                dots = work.tile([P, 4, 2 * P], F32)
                st["dots", m] = dots
            dots = st["dots", m]
            dp = st.pop(("dp", m, half))
            for i in range(2):
                c = 2 * half + i
                k = 4 * (m % 2) + c
                if on_vector("S3" + "ab"[half], m):
                    nc.vector.tensor_scalar(
                        out=dots[:, c, :],
                        in0=dp[:, i, :],
                        scalar1=rl[:, k : k + 1],
                        scalar2=pr[:, k : k + 1],
                        op0=ALU.mult,
                        op1=ALU.add,
                    )
                else:
                    nc.scalar.activation(
                        out=dots[:, c, :],
                        in_=dp[:, i, :],
                        func=ACT.Identity,
                        scale=rl[:, k : k + 1],
                        bias=pr[:, k : k + 1],
                    )

        def turn_out(m, j):
            oT = ps_o.tile([P, 4, P], F32)
            for c in range(4):
                nc.tensor.transpose(oT[:, c, :], st["dots", m][:, c, P * j : P * (j + 1)], ident[:])
            st["oT", m, j] = oT

        def exit_out(m, j):
            if ("o", m) not in st:
                o_sb = work.tile([P, 2, C], F32)
                st["o", m] = [o_sb, 0]
            o_sb = st["o", m][0]
            copy_out("X3" + "ab"[j], m, o_sb[:, j, :], st.pop(("oT", m, j))[:].rearrange("p c j -> p (c j)"))
            st["o", m][1] += 1
            s, h = m // 2, m % 2
            rows = out[h].rearrange("(p a) c -> p a c", a=N_TILES)
            if m >= N_TILES - 2:
                nc.sync.dma_start(out=rows[:, 2 * s + j, :], in_=o_sb[:, j, :])
            elif st["o", m][1] == 2:
                nc.sync.dma_start(out=rows[:, 2 * s : 2 * s + 2, :], in_=o_sb[:])

        run = {
            "prod": prod, "T1": turn_x, "X1": exit_x, "Q1": quant_x,
            "M1a": lambda n: project(n, 0), "M1b": lambda n: project(n, 1),
            "V2a": lambda n: add_bias(n, 0), "V2b": lambda n: add_bias(n, 1),
            "SQa": lambda n: square(n, 0), "SQb": lambda n: square(n, 1),
            "RS": root,
            "V3a": lambda m: normalise(m, 0), "V3b": lambda m: normalise(m, 1),
            "T2": turn_u, "X2": exit_u, "Q2": quant_u,
            "M2a": lambda m: compare(m, 0), "M2b": lambda m: compare(m, 1),
            "S3a": lambda m: scale_out(m, 0), "S3b": lambda m: scale_out(m, 1),
            "T3a": lambda m: turn_out(m, 0), "T3b": lambda m: turn_out(m, 1),
            "X3a": lambda m: exit_out(m, 0), "X3b": lambda m: exit_out(m, 1),
        }
        lags = [lag for name, lag in TABLE]
        for it in range(min(lags), N_TILES + max(lags)):
            if it == 1:
                constants()
            for name, lag in TABLE:
                if 0 <= it - lag < N_TILES:
                    run[name](it - lag)
